import numpy as np
import ml_dtypes

BF16 = ml_dtypes.bfloat16


def bf(x):
    return np.asarray(x, np.float32).astype(BF16)


def f32(x):
    return np.asarray(x, np.float32)


def f64(x):
    return np.asarray(x).astype(np.float64)


def striped(idx):
    return np.tile(idx.reshape(-1, 16).T, (8, 1))


def rows(idx, k):
    return np.tile(idx, (k, 1))


def look(tab, idx):
    return np.take_along_axis(f64(tab), rows(idx, len(tab)), axis=1)


K, S, H, V, N = 128, 2048, 256, 1536, 1536


def setup_inputs():
    return {"z": bf(np.random.standard_normal((H, S))), "wt": bf(np.random.standard_normal((H, K)) / np.sqrt(H)), "base": f32(1.0 * np.random.standard_normal((K, V))), "offs": striped(np.random.permutation(S)[:N])}


def reference(z, wt, base, offs):
    idx = offs[:16].T.reshape(-1)
    tab = f64(wt).T @ f64(z)
    x = f64(base) + look(tab, idx)
    return x

@@ -1,0 +1,53 @@
+import concourse.mybir as mybir
+
+K, R, S, N = 256, 128, 2048, 1536
+FLOPS = 2 * K * R * S + R * N
+
+P = 128
+BANK = 512
+PIECE = 512
+PER_COLUMN = 16
+F32, BF16, U16 = mybir.dt.float32, mybir.dt.bfloat16, mybir.dt.uint16
+
+
+def tile_lookup_pjadd_out_kernel(tc, z, wt, base, offs, out):
+    nc = tc.nc
+    halves = K // P
+    z_view = z.rearrange("(p c) s -> p c s", c=halves)
+    wt_view = wt.rearrange("(p c) r -> p c r", c=halves)
+
+    with (
+        tc.tile_pool(name="held", bufs=1) as held,
+        tc.tile_pool(name="features", bufs=S // BANK) as features,
+        tc.tile_pool(name="stream", bufs=N // PIECE) as stream,
+        tc.tile_pool(name="result", bufs=N // PIECE) as result,
+        tc.psum_pool(name="psum", bufs=S // BANK) as psum,
+    ):
+        weights = held.tile([P, halves, R], BF16)
+        table = held.tile([P, S], F32)
+        offsets = held.tile([P, N // PER_COLUMN], U16)
+
+        nc.scalar.dma_start(weights[:], wt_view)
+
+        for b in range(S // BANK):
+            places = slice(b * BANK, (b + 1) * BANK)
+            block = features.tile([P, halves, BANK], BF16)
+            nc.sync.dma_start(block[:], z_view[:, :, places])
+            projected = psum.tile([P, BANK], F32)
+            for c in range(halves):
+                nc.tensor.matmul(projected[:], weights[:, c, :], block[:, c, :], start=(c == 0), stop=(c == halves - 1))
+            if b % 2 == 0:
+                nc.scalar.copy(table[:, places], projected[:])
+            else:
+                nc.vector.tensor_copy(table[:, places], projected[:])
+
+        nc.sync.dma_start(offsets[:], offs)
+
+        for i in range(N // PIECE):
+            entries = slice(i * PIECE, (i + 1) * PIECE)
+            columns = slice(i * PIECE // PER_COLUMN, (i + 1) * PIECE // PER_COLUMN)
+            base_piece = stream.tile([P, PIECE], F32)
+            nc.sync.dma_start(base_piece[:], base[:, entries])
+            x = result.tile([P, PIECE], F32)
+            nc.vector.tensor_tensor(x[:], table[:].indirect(offsets[:, columns]), base_piece[:], mybir.AluOpType.add)
+            nc.sync.dma_start(out[:, entries], x[:])

@@ -4,8 +4,10 @@ K, R, S, N = 256, 128, 2048, 1536
 FLOPS = 2 * K * R * S + R * N
 
 P = 128
-BANK = 512
+BLOCK = 512
+HALF = BLOCK // 2
 PIECE = 512
+WARM_UP = 10
 PER_COLUMN = 16
 F32, BF16, U16 = mybir.dt.float32, mybir.dt.bfloat16, mybir.dt.uint16
 
@@ -18,10 +20,10 @@ def tile_lookup_pjadd_out_kernel(tc, z, wt, base, offs, out):
 
     with (
         tc.tile_pool(name="held", bufs=1) as held,
-        tc.tile_pool(name="features", bufs=S // BANK) as features,
+        tc.tile_pool(name="features", bufs=S // BLOCK) as features,
         tc.tile_pool(name="stream", bufs=N // PIECE) as stream,
         tc.tile_pool(name="result", bufs=N // PIECE) as result,
-        tc.psum_pool(name="psum", bufs=S // BANK) as psum,
+        tc.psum_pool(name="psum", bufs=S // HALF) as psum,
     ):
         weights = held.tile([P, halves, R], BF16)
         table = held.tile([P, S], F32)
@@ -29,17 +31,30 @@ def tile_lookup_pjadd_out_kernel(tc, z, wt, base, offs, out):
 
         nc.scalar.dma_start(weights[:], wt_view)
 
-        for b in range(S // BANK):
-            places = slice(b * BANK, (b + 1) * BANK)
-            block = features.tile([P, halves, BANK], BF16)
-            nc.sync.dma_start(block[:], z_view[:, :, places])
-            projected = psum.tile([P, BANK], F32)
-            for c in range(halves):
-                nc.tensor.matmul(projected[:], weights[:, c, :], block[:, c, :], start=(c == 0), stop=(c == halves - 1))
-            if b % 2 == 0:
-                nc.scalar.copy(table[:, places], projected[:])
-            else:
-                nc.vector.tensor_copy(table[:, places], projected[:])
+        zeros = held.tile([P, HALF], BF16)
+        nc.vector.memset(zeros[:], 0.0)
+        idle = psum.tile([P, HALF], F32, tag="projected")
+        for n in range(WARM_UP):
+            nc.tensor.matmul(idle[:], zeros[:, :P], zeros[:], start=True, stop=True)
+
+        for b in range(S // BLOCK):
+            block = features.tile([P, halves, BLOCK], BF16)
+            nc.sync.dma_start(block[:], z_view[:, :, b * BLOCK : (b + 1) * BLOCK])
+            for h in range(BLOCK // HALF):
+                projected = psum.tile([P, HALF], F32)
+                for c in range(halves):
+                    nc.tensor.matmul(
+                        projected[:],
+                        weights[:, c, :],
+                        block[:, c, h * HALF : (h + 1) * HALF],
+                        start=(c == 0),
+                        stop=(c == halves - 1),
+                    )
+                places = slice(b * BLOCK + h * HALF, b * BLOCK + (h + 1) * HALF)
+                if h % 2 == 0:
+                    nc.scalar.copy(table[:, places], projected[:])
+                else:
+                    nc.vector.tensor_copy(table[:, places], projected[:])
 
         nc.sync.dma_start(offsets[:], offs)
 

@@ -7,7 +7,7 @@ P = 128
 BLOCK = 512
 HALF = BLOCK // 2
 PIECE = 512
-WARM_UP = 10
+WARM_UP = 7
 PER_COLUMN = 16
 F32, BF16, U16 = mybir.dt.float32, mybir.dt.bfloat16, mybir.dt.uint16
 
@@ -21,8 +21,8 @@ def tile_lookup_pjadd_out_kernel(tc, z, wt, base, offs, out):
     with (
         tc.tile_pool(name="held", bufs=1) as held,
         tc.tile_pool(name="features", bufs=S // BLOCK) as features,
-        tc.tile_pool(name="stream", bufs=N // PIECE) as stream,
-        tc.tile_pool(name="result", bufs=N // PIECE) as result,
+        tc.tile_pool(name="stream", bufs=N // PIECE + 1) as stream,
+        tc.tile_pool(name="result", bufs=N // PIECE + 1) as result,
         tc.psum_pool(name="psum", bufs=S // HALF) as psum,
     ):
         weights = held.tile([P, halves, R], BF16)
@@ -58,11 +58,11 @@ def tile_lookup_pjadd_out_kernel(tc, z, wt, base, offs, out):
 
         nc.sync.dma_start(offsets[:], offs)
 
-        for i in range(N // PIECE):
-            entries = slice(i * PIECE, (i + 1) * PIECE)
-            columns = slice(i * PIECE // PER_COLUMN, (i + 1) * PIECE // PER_COLUMN)
-            base_piece = stream.tile([P, PIECE], F32)
-            nc.sync.dma_start(base_piece[:], base[:, entries])
-            x = result.tile([P, PIECE], F32)
-            nc.vector.tensor_tensor(x[:], table[:].indirect(offsets[:, columns]), base_piece[:], mybir.AluOpType.add)
-            nc.sync.dma_start(out[:, entries], x[:])
+        cuts = list(range(0, N, PIECE)) + [N - PIECE // 2, N]
+        for first, last in zip(cuts, cuts[1:]):
+            base_piece = stream.tile([P, last - first], F32)
+            nc.sync.dma_start(base_piece[:], base[:, first:last])
+            x = result.tile([P, last - first], F32)
+            picked = table[:].indirect(offsets[:, first // PER_COLUMN : last // PER_COLUMN])
+            nc.vector.tensor_tensor(x[:], picked, base_piece[:], mybir.AluOpType.add)
+            nc.sync.dma_start(out[:, first:last], x[:])

@@ -6,6 +6,7 @@ FLOPS = 2 * K * R * S + R * N
 P = 128
 BLOCK = 512
 HALF = BLOCK // 2
+PSUM_BANKS = 8
 PIECE = 512
 WARM_UP = 7
 PER_COLUMN = 16
@@ -20,10 +21,10 @@ def tile_lookup_pjadd_out_kernel(tc, z, wt, base, offs, out):
 
     with (
         tc.tile_pool(name="held", bufs=1) as held,
-        tc.tile_pool(name="features", bufs=S // BLOCK) as features,
+        tc.tile_pool(name="features", bufs=S // BLOCK + 1) as features,
         tc.tile_pool(name="stream", bufs=N // PIECE + 1) as stream,
         tc.tile_pool(name="result", bufs=N // PIECE + 1) as result,
-        tc.psum_pool(name="psum", bufs=S // HALF) as psum,
+        tc.psum_pool(name="psum", bufs=PSUM_BANKS) as psum,
     ):
         weights = held.tile([P, halves, R], BF16)
         table = held.tile([P, S], F32)
@@ -37,21 +38,20 @@ def tile_lookup_pjadd_out_kernel(tc, z, wt, base, offs, out):
         for n in range(WARM_UP):
             nc.tensor.matmul(idle[:], zeros[:, :P], zeros[:], start=True, stop=True)
 
-        for b in range(S // BLOCK):
-            block = features.tile([P, halves, BLOCK], BF16)
-            nc.sync.dma_start(block[:], z_view[:, :, b * BLOCK : (b + 1) * BLOCK])
-            for h in range(BLOCK // HALF):
-                projected = psum.tile([P, HALF], F32)
+        ends = list(range(0, S, BLOCK)) + [S - HALF, S]
+        for start, end in zip(ends, ends[1:]):
+            size = end - start
+            block = features.tile([P, halves, size], BF16)
+            nc.sync.dma_start(block[:], z_view[:, :, start:end])
+            for h in range(2):
+                part = slice(h * size // 2, (h + 1) * size // 2)
+                projected = psum.tile([P, size // 2], F32)
                 for c in range(halves):
                     nc.tensor.matmul(
-                        projected[:],
-                        weights[:, c, :],
-                        block[:, c, h * HALF : (h + 1) * HALF],
-                        start=(c == 0),
-                        stop=(c == halves - 1),
+                        projected[:], weights[:, c, :], block[:, c, part], start=(c == 0), stop=(c == halves - 1)
                     )
-                places = slice(b * BLOCK + h * HALF, b * BLOCK + (h + 1) * HALF)
-                if h % 2 == 0:
+                places = slice(start + part.start, start + part.stop)
+                if h == 0:
                     nc.scalar.copy(table[:, places], projected[:])
                 else:
                     nc.vector.tensor_copy(table[:, places], projected[:])

import concourse.mybir as mybir

K, R, S, N = 256, 128, 2048, 1536
FLOPS = 2 * K * R * S + R * N

P = 128
BLOCK = 512
HALF = BLOCK // 2
PSUM_BANKS = 8
PIECE = 512
WARM_UP = 7
PER_COLUMN = 16
F32, BF16, U16 = mybir.dt.float32, mybir.dt.bfloat16, mybir.dt.uint16


def tile_lookup_pjadd_out_kernel(tc, z, wt, base, offs, out):
    nc = tc.nc
    halves = K // P
    z_view = z.rearrange("(p c) s -> p c s", c=halves)
    wt_view = wt.rearrange("(p c) r -> p c r", c=halves)

    with (
        tc.tile_pool(name="held", bufs=1) as held,
        tc.tile_pool(name="features", bufs=S // BLOCK + 1) as features,
        tc.tile_pool(name="stream", bufs=N // PIECE + 1) as stream,
        tc.tile_pool(name="result", bufs=N // PIECE + 1) as result,
        tc.psum_pool(name="psum", bufs=PSUM_BANKS) as psum,
    ):
        weights = held.tile([P, halves, R], BF16)
        table = held.tile([P, S], F32)
        offsets = held.tile([P, N // PER_COLUMN], U16)

        nc.scalar.dma_start(weights[:], wt_view)

        zeros = held.tile([P, HALF], BF16)
        nc.vector.memset(zeros[:], 0.0)
        idle = psum.tile([P, HALF], F32, tag="projected")
        for n in range(WARM_UP):
            nc.tensor.matmul(idle[:], zeros[:, :P], zeros[:], start=True, stop=True)

        ends = list(range(0, S, BLOCK)) + [S - HALF, S]
        for start, end in zip(ends, ends[1:]):
            size = end - start
            block = features.tile([P, halves, size], BF16)
            nc.sync.dma_start(block[:], z_view[:, :, start:end])
            for h in range(2):
                part = slice(h * size // 2, (h + 1) * size // 2)
                projected = psum.tile([P, size // 2], F32)
                for c in range(halves):
                    nc.tensor.matmul(
                        projected[:], weights[:, c, :], block[:, c, part], start=(c == 0), stop=(c == halves - 1)
                    )
                places = slice(start + part.start, start + part.stop)
                if h == 0:
                    nc.scalar.copy(table[:, places], projected[:])
                else:
                    nc.vector.tensor_copy(table[:, places], projected[:])

        nc.sync.dma_start(offsets[:], offs)

        cuts = list(range(0, N, PIECE)) + [N - PIECE // 2, N]
        for first, last in zip(cuts, cuts[1:]):
            base_piece = stream.tile([P, last - first], F32)
            nc.sync.dma_start(base_piece[:], base[:, first:last])
            x = result.tile([P, last - first], F32)
            picked = table[:].indirect(offsets[:, first // PER_COLUMN : last // PER_COLUMN])
            nc.vector.tensor_tensor(x[:], picked, base_piece[:], mybir.AluOpType.add)
            nc.sync.dma_start(out[:, first:last], x[:])
